import numpy as np
import ml_dtypes


def mxq(x, axis, fmt="e4m3"):
    dtype, down = {"e4m3": (ml_dtypes.float8_e4m3fn, 7), "e5m2": (ml_dtypes.float8_e5m2, 14)}[fmt]
    v = np.moveaxis(np.asarray(x, np.float32).astype(ml_dtypes.bfloat16).astype(np.float64), axis, -1)
    blocks = v.reshape(v.shape[:-1] + (-1, 32))
    amax = np.abs(blocks).max(-1, keepdims=True)
    byte = np.maximum(np.where(amax > 0, np.frexp(amax)[1] - 1 + 127, 0) - down, 1)
    scale = np.exp2(byte - 127.0)
    codes = (blocks / scale).astype(np.float32).astype(dtype).astype(np.float64)
    return np.moveaxis((codes * scale).reshape(v.shape), -1, axis)


WIDE = False


def mx_kscale(k):
    if not WIDE:
        return np.ones(k)
    levels = np.array([10, -10, 5, -5, 0])
    if k % 512:
        return np.exp2(np.random.permutation(np.resize(levels, k // 32))).repeat(32)
    a = np.empty((k // 512, 16))
    for p in range(k // 512):
        a[p, :8] = np.random.permutation(np.resize(levels, 8))
        for g in range(8):
            far = levels[np.abs(levels - a[p, g]) >= 10]
            a[p, g + 8] = far[np.random.randint(len(far))]
    return np.exp2(a.ravel()).repeat(32)


def f64(x):
    return np.asarray(x).astype(np.float64)


def striped(idx):
    return np.tile(np.asarray(idx).reshape(-1, 16).T, (8, 1)).astype(np.uint16)


def unstriped(offs):
    return offs[:16].T.reshape(-1).astype(np.int64)


E2M1 = np.array([0.0, 0.5, 1.0, 1.5, 2.0, 3.0, 4.0, 6.0, -0.0, -0.5, -1.0, -1.5, -2.0, -3.0, -4.0, -6.0])


def pack_weight(w, fmt):
    k, n = w.shape
    w = f64(np.asarray(w, np.float32).astype(ml_dtypes.bfloat16)).reshape(k // 32, 32, n)
    amax = np.abs(w).max(1)
    if fmt == "e4m3":
        byte = np.frexp(amax)[1] - 1 + 127 - 7
    else:
        mant, ex = np.frexp(amax / 6.0)
        byte = np.where(mant > 0.5, ex, ex - 1) + 127
    byte = np.clip(np.where(amax > 0, byte, 1), 1, 254)
    scaled = (w * np.exp2(127.0 - byte)[:, None, :]).reshape(k, n).astype(np.float32)
    by_word = np.ascontiguousarray(scaled.reshape(k // 512, 128, 4, n).transpose(0, 1, 3, 2))
    if fmt == "e4m3":
        words = by_word.astype(ml_dtypes.float8_e4m3fn).view(np.uint8)
    else:
        c = by_word.astype(ml_dtypes.float4_e2m1fn).view(np.uint8) & 0xF
        words = (c[..., 0::2] | (c[..., 1::2] << 4)).reshape(k // 512, 128, 2 * n)
    return np.ascontiguousarray(words), np.ascontiguousarray(byte.astype(np.uint8).reshape(k // 512, 16, n))


def unpack_weight(words, scales, fmt):
    g, _, n = scales.shape
    words = np.ascontiguousarray(words).reshape(g, 128, n, -1)
    if fmt == "e4m3":
        vals = words.view(ml_dtypes.float8_e4m3fn).astype(np.float64)
    else:
        nib = np.empty((g, 128, n, 4), np.uint8)
        nib[..., 0::2] = words & 0xF
        nib[..., 1::2] = words >> 4
        vals = E2M1[nib]
    vals = vals * np.repeat(np.exp2(scales.astype(np.float64) - 127.0), 8, axis=1)[..., None]
    return vals.transpose(0, 1, 3, 2).reshape(g * 512, n)


def sigmoid(v):
    return 1.0 / (1.0 + np.exp(-v))


def bf(x):
    return np.asarray(x, np.float32).astype(ml_dtypes.bfloat16)


def planes(Y):
    r, m = Y.shape
    b = f64(bf(Y)).reshape(r // 32, 32, m)
    amax = np.abs(b).max(1)
    byte = np.clip(np.where(amax > 0, np.frexp(amax)[1] - 1 + 127 - 7, 1), 1, 254)
    codes = (b * np.exp2(127.0 - byte)[:, None, :]).reshape(r, m).astype(np.float32).astype(ml_dtypes.float8_e4m3fn).view(np.uint8)
    words = codes.reshape(r // 512, 128, 4, m).transpose(0, 1, 3, 2)
    return np.ascontiguousarray(words), np.ascontiguousarray(byte.astype(np.uint8).reshape(r // 512, 16, m))


D, E, T, I, Q = 512, 512, 1024, 256, 128


def setup_inputs():
    n = np.random.standard_normal
    idx = np.random.permutation(T)[:I]
    idx2 = np.random.permutation(T)[:I]
    fd = mx_kscale(D)
    fe = mx_kscale(E)
    keysp = pack_weight(n((D, T)) / fd[:, None], "e4m3")
    pvp = pack_weight(n((E, T)) / fe[:, None], "e4m3")
    return {
        "query": (n((D, Q)) * 1.0 / np.sqrt(D) * fd[:, None]).astype(np.float32),
        "keys_words": keysp[0],
        "keys_scales": keysp[1],
        "bias": (np.random.uniform(-1.0, 1.0, (I, 1))).astype(np.float32),
        "half": (np.random.uniform(0.3, 2.0, (I, 1))).astype(np.float32),
        "vals": (n((E, T)) * np.random.uniform(0.3, 1.5, (1, T))).astype(np.float32),
        "sval": (n((E, T)) * 0.7).astype(np.float32),
        "gout": (n((E, Q)) * 1 / np.sqrt(E) * fe[:, None]).astype(np.float32),
        "pv_words": pvp[0],
        "pv_scales": pvp[1],
        "old": (n((E, T)) * 0.1).astype(np.float32),
        "offs": striped(idx),
        "offs2": striped(idx2),
    }


def reference(query, keys_words, keys_scales, bias, half, vals, sval, gout, pv_words, pv_scales, old, offs, offs2):
    idx = unstriped(offs)
    idx2 = unstriped(offs2)
    keysu = unpack_weight(keys_words, keys_scales, "e4m3")
    pvu = unpack_weight(pv_words, pv_scales, "e4m3")
    keysidxg = keysu[:, idx]
    queryq = mxq(f64(query), 0, "e4m3")
    a = keysidxg.T @ queryq
    va = f64(vals)[:, idx].T
    vb = f64(sval)[:, idx2].T
    df1 = va - vb
    nv = np.mean(np.square(df1), axis=1, keepdims=True)
    pvidxg = pvu[:, idx]
    goutq = mxq(f64(gout), 0, "e4m3")
    c0 = pvidxg.T @ goutq
    dnf = np.sum(c0 * sigmoid(a + f64(bias)), axis=1, keepdims=True)
    dnv = dnf / (nv + f64(half)) - dnf * nv / np.square(nv + f64(half))
    ddf1 = dnv / 512.0 * df1 * 2.0
    dvb = ddf1 * (-1.0)
    g1 = dvb * 16.0
    g2 = g1.T
    gf = np.zeros((E, T))
    gf[:, idx2] = g2
    y = f64(old) + gf
    words, scales = planes(y)
    return y, words, scales

@@ -1,0 +1,211 @@
+from contextlib import ExitStack
+
+import concourse.mybir as mybir
+from concourse.masks import make_identity
+
+F32 = mybir.dt.float32
+BF16 = mybir.dt.bfloat16
+I32 = mybir.dt.int32
+U32 = mybir.dt.uint32
+U16 = mybir.dt.uint16
+U8 = mybir.dt.uint8
+FP8X4 = mybir.dt.float8_e4m3fn_x4
+ALU = mybir.AluOpType
+ACT = mybir.ActivationFunctionType
+
+P = 128
+PACK = 4
+T = 1024
+SLOTS = 256
+Q = 128
+HALVES = SLOTS // P
+CHUNKS = [(0, 256), (256, 512), (512, 768), (768, 896), (896, 1024)]
+
+FLOPS = 2 * 2 * 512 * SLOTS * Q
+
+
+def tile_attend_bnovelty_pl_kernel(tc, query, keys_words, keys_scales, bias, half, vals, sval, gout,
+                                    pv_words, pv_scales, old, offs, offs2, out_0, out_1, out_2):
+    nc = tc.nc
+    with ExitStack() as ctx:
+        sb = ctx.enter_context(tc.tile_pool(name="sb", bufs=1))
+        ps = ctx.enter_context(tc.psum_pool(name="ps", bufs=1))
+
+        def planes(x):
+            return x.rearrange("(p j) t -> p j t", j=PACK)
+
+        list1 = sb.tile([P, SLOTS // 16], U16, name="list1")
+        list2 = sb.tile([P, SLOTS // 16], U16, name="list2")
+        vals_sb = [sb.tile([P, T], F32, name="vals%d" % j) for j in range(PACK)]
+        sval_sb = [sb.tile([P, T], F32, name="sval%d" % j) for j in range(PACK)]
+        gf = [sb.tile([P, T], F32, name="gf%d" % j) for j in range(PACK)]
+        y = [sb.tile([P, 2, T], F32, name="y%d" % u) for u in range(2)]
+        q_raw = sb.tile([P, PACK, Q], F32, name="q_raw")
+        g_raw = sb.tile([P, PACK, Q], F32, name="g_raw")
+        bias_sb = sb.tile([P, HALVES], F32, name="bias_sb")
+        half_sb = sb.tile([P, HALVES], F32, name="half_sb")
+        kw = sb.tile([P, T], I32, name="kw")
+        pw = sb.tile([P, T], I32, name="pw")
+        ks = sb.tile([P, T], U8, name="ks")
+        pvs = sb.tile([P, T], U8, name="pvs")
+        ident = sb.tile([P, P], F32, name="ident")
+        warm_in = sb.tile([P, 1], F32, name="warm_in")
+        warm_out = sb.tile([P, 1], F32, name="warm_out")
+
+        nc.gpsimd.memset(ks[:].bitcast(I32), 0)
+        nc.gpsimd.memset(pvs[:].bitcast(I32), 0)
+        nc.gpsimd.memset(warm_in[:], 0.0)
+        nc.scalar.activation(warm_out[:], warm_in[:], ACT.Sigmoid)
+        make_identity(nc, ident[:])
+        for j in range(PACK):
+            engine = nc.vector if j < 2 else nc.gpsimd
+            engine.memset(gf[j][:], 0.0)
+
+        def load_scale_rows(tile, src, quad):
+            nc.sync.dma_start(tile[32 * quad:32 * quad + 4, :].bitcast(I32),
+                              src[0, 4 * quad:4 * quad + 4, :].bitcast(I32))
+
+        def load_column(tile, src):
+            with nc.allow_non_contiguous_dma(reason="one value of each half of the slots to a partition"):
+                nc.sync.dma_start(tile[:], src.rearrange("(h p) o -> p (h o)", p=P))
+
+        nc.sync.dma_start(list1[:], offs)
+        nc.sync.dma_start(list2[:], offs2)
+        nc.sync.dma_start(vals_sb[0][:], planes(vals)[:, 0, :])
+        load_column(half_sb, half)
+        nc.sync.dma_start(sval_sb[0][:], planes(sval)[:, 0, :])
+        load_column(bias_sb, bias)
+        big = [(q_raw, planes(query)), (g_raw, planes(gout))]
+        for j in range(1, PACK):
+            big = big + [(vals_sb[j], planes(vals)[:, j, :]), (sval_sb[j], planes(sval)[:, j, :])]
+        small = [(ks, keys_scales, quad) for quad in range(4)] + [(pvs, pv_scales, quad) for quad in range(4)]
+        load_scale_rows(*small[0])
+        for n, (tile, src) in enumerate(big):
+            nc.sync.dma_start(tile[:], src)
+            if n + 1 < len(small):
+                load_scale_rows(*small[n + 1])
+        nc.sync.dma_start(kw[:], keys_words[0].rearrange("p n t -> p (n t)").bitcast(I32))
+        nc.sync.dma_start(pw[:], pv_words[0].rearrange("p n t -> p (n t)").bitcast(I32))
+        for j in range(PACK):
+            nc.sync.dma_start(y[j // 2][:, j % 2, :], planes(old)[:, j, :])
+
+        qg = sb.tile([P, 2, Q, PACK], BF16, name="qg", align_bytes=64)
+        qg_words = sb.tile([P, 2 * Q], U32, name="qg_words", align_bytes=64)
+        qg_scales = sb.tile([P, 2 * Q], U8, name="qg_scales", align_bytes=64)
+        nc.scalar.copy(qg[:, 0, :, :], q_raw[:].rearrange("p j q -> p q j"))
+        nc.scalar.copy(qg[:, 1, :, :], g_raw[:].rearrange("p j q -> p q j"))
+        half4 = sb.tile([P, HALVES], F32, name="half4")
+        nc.gpsimd.tensor_scalar(half4[:], half_sb[:], 4.0, 0.0, ALU.mult, ALU.add)
+
+        va = [sb.tile([P, SLOTS], F32, name="va%d" % j) for j in range(PACK)]
+        diff = [sb.tile([P, SLOTS], F32, name="diff%d" % j) for j in range(PACK)]
+        diff_t = [ps.tile([P, PACK, P], F32, name="diff_t%d" % h) for h in range(HALVES)]
+        ksg = sb.tile([P, SLOTS], U8, name="ksg", align_bytes=64)
+        psg = sb.tile([P, SLOTS], U8, name="psg", align_bytes=64)
+        kwg = sb.tile([P, SLOTS], U32, name="kwg", align_bytes=64)
+        pwg = sb.tile([P, SLOTS], U32, name="pwg", align_bytes=64)
+        squares = sb.tile([P, 3 * P], F32, name="squares")
+        early = sb.tile([P, HALVES], F32, name="early")
+        base = sb.tile([P, HALVES], F32, name="base")
+        for j in range(PACK):
+            nc.vector.tensor_copy(va[j][:], vals_sb[j][:].indirect(list1[:]))
+            if j == 2:
+                nc.vector.tensor_copy(ksg[:], ks[:].indirect(list1[:]))
+            if j == 3:
+                nc.vector.tensor_copy(psg[:], pvs[:].indirect(list1[:]))
+            nc.vector.tensor_tensor(diff[j][:], sval_sb[j][:].indirect(list2[:]), va[j][:], ALU.subtract)
+            for h in range(HALVES):
+                nc.tensor.transpose(diff_t[h][:, j, :], diff[j][:, h * P:(h + 1) * P], ident[:])
+            if j == 0:
+                nc.vector.quantize_mx(out=qg_words[:].bitcast(FP8X4), scales=qg_scales[:],
+                                      in_=qg[:].rearrange("p a q j -> p (a q j)"))
+            if j == 2:
+                for h in range(HALVES):
+                    nc.scalar.activation(squares[:, 0:3 * P], diff_t[h][:, 0:3, :].rearrange("p j e -> p (j e)"),
+                                         ACT.Square, accum_out=early[:, h:h + 1])
+                for h in range(HALVES):
+                    nc.scalar.activation(base[:, h:h + 1], early[:, h:h + 1], ACT.Identity,
+                                         bias=half4[:, h:h + 1], scale=1.0 / 128.0)
+        nc.vector.tensor_copy(kwg[:], kw[:].bitcast(U32).indirect(list1[:]))
+
+        sumsq = sb.tile([P, HALVES], F32, name="sumsq")
+        denom = sb.tile([P, HALVES], F32, name="denom")
+        for h in range(HALVES):
+            nc.scalar.activation(squares[:, 0:P], diff_t[h][:, 3, :], ACT.Square, accum_out=sumsq[:, h:h + 1])
+        for h in range(HALVES):
+            nc.scalar.activation(denom[:, h:h + 1], sumsq[:, h:h + 1], ACT.Square,
+                                 bias=base[:, h:h + 1], scale=1.0 / 128.0)
+
+        score = ps.tile([P, HALVES, Q], F32, name="score")
+        for h in range(HALVES):
+            nc.tensor.matmul_mx(out=score[:, h, :], lhsT=kwg[:, h * P:(h + 1) * P].bitcast(FP8X4),
+                                lhsT_scale=ksg[:, h * P:(h + 1) * P],
+                                rhs=qg_words[:, 0:Q].bitcast(FP8X4), rhs_scale=qg_scales[:, 0:Q],
+                                start=True, stop=True)
+        gate = sb.tile([P, HALVES, Q], F32, name="gate")
+        for h in range(HALVES):
+            nc.scalar.activation(gate[:, h, :], score[:, h, :], ACT.Sigmoid, bias=bias_sb[:, h:h + 1])
+
+        inv = sb.tile([P, HALVES], F32, name="inv")
+        factor = sb.tile([P, HALVES], F32, name="factor")
+        nc.vector.reciprocal(inv[:], denom[:])
+        nc.vector.tensor_tensor(factor[:], inv[:], half_sb[:], ALU.mult)
+
+        cols = SLOTS // 16 // HALVES
+        dread = [ps.tile([P, Q], F32, name="dread%d" % h) for h in range(HALVES)]
+        for h in range(HALVES):
+            nc.vector.tensor_copy(pwg[:, h * P:(h + 1) * P],
+                                  pw[:].bitcast(U32).indirect(list1[:, h * cols:(h + 1) * cols]))
+            nc.tensor.matmul_mx(out=dread[h][:], lhsT=pwg[:, h * P:(h + 1) * P].bitcast(FP8X4),
+                                lhsT_scale=psg[:, h * P:(h + 1) * P],
+                                rhs=qg_words[:, Q:2 * Q].bitcast(FP8X4), rhs_scale=qg_scales[:, Q:2 * Q],
+                                start=True, stop=True)
+
+        terms = sb.tile([P, Q], F32, name="terms")
+        coef = sb.tile([P, HALVES], F32, name="coef")
+        coef_ps = [ps.tile([P, P], F32, name="coef_ps%d" % h) for h in range(HALVES)]
+        coef_row = sb.tile([P, SLOTS], F32, name="coef_row")
+        for h in range(HALVES):
+            nc.vector.scalar_tensor_tensor(terms[:], dread[h][:], factor[:, h:h + 1], gate[:, h, :],
+                                           ALU.mult, ALU.mult, accum_out=coef[:, h:h + 1])
+            nc.tensor.transpose(coef_ps[h][:], coef[:, h:h + 1].to_broadcast([P, P]), ident[:])
+            nc.scalar.copy(coef_row[:, h * P:(h + 1) * P], coef_ps[h][:])
+
+        yq = [sb.tile([P, c1 - c0, PACK], BF16, name="yq%d" % c0, align_bytes=64) for c0, c1 in CHUNKS]
+        words = [sb.tile([P, c1 - c0], U32, name="words%d" % c0, align_bytes=64) for c0, c1 in CHUNKS]
+        scales = sb.tile([P, T], U8, name="scales", align_bytes=64)
+        out_planes = planes(out_0)
+        out_bytes = out_1[0].rearrange("p n t -> p (n t)")
+
+        for j in range(2):
+            if j == 0:
+                for h in range(HALVES):
+                    nc.vector.tensor_tensor(gf[j][:].indirect(list2[:, h * cols:(h + 1) * cols]),
+                                            diff[j][:, h * P:(h + 1) * P], coef_row[:, h * P:(h + 1) * P], ALU.mult)
+            else:
+                nc.vector.tensor_tensor(gf[j][:].indirect(list2[:]), diff[j][:], coef_row[:], ALU.mult)
+            nc.vector.tensor_tensor(y[0][:, j, :], y[0][:, j, :], gf[j][:], ALU.add)
+            nc.sync.dma_start(out_planes[:, j, :], y[0][:, j, :])
+        for n, (c0, c1) in enumerate(CHUNKS):
+            nc.scalar.copy(yq[n][:, :, 0:2], y[0][:, :, c0:c1].rearrange("p j t -> p t j"))
+        for j in range(2, 4):
+            nc.vector.tensor_tensor(gf[j][:].indirect(list2[:]), diff[j][:], coef_row[:], ALU.mult)
+
+        def quantise(n):
+            c0, c1 = CHUNKS[n]
+            nc.vector.quantize_mx(out=words[n][:].bitcast(FP8X4), scales=scales[:, c0:c1],
+                                  in_=yq[n][:].rearrange("p t j -> p (t j)"))
+            nc.sync.dma_start(out_bytes[:, PACK * c0:PACK * c1].bitcast(I32), words[n][:].bitcast(I32))
+
+        for n, (c0, c1) in enumerate(CHUNKS):
+            for j in range(2):
+                nc.vector.tensor_tensor(y[1][:, j, c0:c1], y[1][:, j, c0:c1], gf[2 + j][:, c0:c1], ALU.add)
+            nc.scalar.copy(yq[n][:, :, 2:4], y[1][:, :, c0:c1].rearrange("p j t -> p t j"))
+            nc.sync.dma_start(out_planes[:, 2:4, c0:c1], y[1][:, :, c0:c1])
+            if n > 0:
+                quantise(n - 1)
+        quantise(len(CHUNKS) - 1)
+        for quad in range(4):
+            queue = nc.sync if quad % 2 == 0 else nc.scalar
+            queue.dma_start(out_2[0, 4 * quad:4 * quad + 4, :].bitcast(I32),
+                            scales[32 * quad:32 * quad + 4, :].bitcast(I32))

@@ -19,7 +19,7 @@ T = 1024
 SLOTS = 256
 Q = 128
 HALVES = SLOTS // P
-CHUNKS = [(0, 256), (256, 512), (512, 768), (768, 896), (896, 1024)]
+CHUNKS = [(0, 256), (256, 512), (512, 768), (768, 1024)]
 
 FLOPS = 2 * 2 * 512 * SLOTS * Q
 
@@ -42,8 +42,10 @@ def tile_attend_bnovelty_pl_kernel(tc, query, keys_words, keys_scales, bias, hal
         y = [sb.tile([P, 2, T], F32, name="y%d" % u) for u in range(2)]
         q_raw = sb.tile([P, PACK, Q], F32, name="q_raw")
         g_raw = sb.tile([P, PACK, Q], F32, name="g_raw")
-        bias_sb = sb.tile([P, HALVES], F32, name="bias_sb")
-        half_sb = sb.tile([P, HALVES], F32, name="half_sb")
+        rows = sb.tile([P, P], F32, name="rows")
+        columns = sb.tile([P, 2 * HALVES], F32, name="columns")
+        bias_sb = columns[:, 0:HALVES]
+        half_sb = columns[:, HALVES:2 * HALVES]
         kw = sb.tile([P, T], I32, name="kw")
         pw = sb.tile([P, T], I32, name="pw")
         ks = sb.tile([P, T], U8, name="ks")
@@ -55,6 +57,7 @@ def tile_attend_bnovelty_pl_kernel(tc, query, keys_words, keys_scales, bias, hal
         nc.gpsimd.memset(ks[:].bitcast(I32), 0)
         nc.gpsimd.memset(pvs[:].bitcast(I32), 0)
         nc.gpsimd.memset(warm_in[:], 0.0)
+        nc.gpsimd.memset(rows[:], 0.0)
         nc.scalar.activation(warm_out[:], warm_in[:], ACT.Sigmoid)
         make_identity(nc, ident[:])
         for j in range(PACK):
@@ -65,37 +68,41 @@ def tile_attend_bnovelty_pl_kernel(tc, query, keys_words, keys_scales, bias, hal
             nc.sync.dma_start(tile[32 * quad:32 * quad + 4, :].bitcast(I32),
                               src[0, 4 * quad:4 * quad + 4, :].bitcast(I32))
 
-        def load_column(tile, src):
-            with nc.allow_non_contiguous_dma(reason="one value of each half of the slots to a partition"):
-                nc.sync.dma_start(tile[:], src.rearrange("(h p) o -> p (h o)", p=P))
-
+        nc.sync.dma_start(vals_sb[0][:], planes(vals)[:, 0, :])
         nc.sync.dma_start(list1[:], offs)
         nc.sync.dma_start(list2[:], offs2)
-        nc.sync.dma_start(vals_sb[0][:], planes(vals)[:, 0, :])
-        load_column(half_sb, half)
-        nc.sync.dma_start(sval_sb[0][:], planes(sval)[:, 0, :])
-        load_column(bias_sb, bias)
-        big = [(q_raw, planes(query)), (g_raw, planes(gout))]
+        big = [(sval_sb[0], planes(sval)[:, 0, :])]
         for j in range(1, PACK):
             big = big + [(vals_sb[j], planes(vals)[:, j, :]), (sval_sb[j], planes(sval)[:, j, :])]
         small = [(ks, keys_scales, quad) for quad in range(4)] + [(pvs, pv_scales, quad) for quad in range(4)]
-        load_scale_rows(*small[0])
         for n, (tile, src) in enumerate(big):
             nc.sync.dma_start(tile[:], src)
-            if n + 1 < len(small):
-                load_scale_rows(*small[n + 1])
+            if n < 4:
+                load_scale_rows(*small[2 * n])
+                load_scale_rows(*small[2 * n + 1])
+            if n == 0:
+                nc.sync.dma_start(q_raw[:], planes(query))
+            if n == 4:
+                nc.sync.dma_start(rows[0:HALVES, :], bias.rearrange("(h p) o -> h (p o)", p=P))
+                nc.sync.dma_start(rows[HALVES:2 * HALVES, :], half.rearrange("(h p) o -> h (p o)", p=P))
+        nc.sync.dma_start(g_raw[:], planes(gout))
         nc.sync.dma_start(kw[:], keys_words[0].rearrange("p n t -> p (n t)").bitcast(I32))
         nc.sync.dma_start(pw[:], pv_words[0].rearrange("p n t -> p (n t)").bitcast(I32))
         for j in range(PACK):
             nc.sync.dma_start(y[j // 2][:, j % 2, :], planes(old)[:, j, :])
 
-        qg = sb.tile([P, 2, Q, PACK], BF16, name="qg", align_bytes=64)
-        qg_words = sb.tile([P, 2 * Q], U32, name="qg_words", align_bytes=64)
-        qg_scales = sb.tile([P, 2 * Q], U8, name="qg_scales", align_bytes=64)
-        nc.scalar.copy(qg[:, 0, :, :], q_raw[:].rearrange("p j q -> p q j"))
-        nc.scalar.copy(qg[:, 1, :, :], g_raw[:].rearrange("p j q -> p q j"))
+        q_bf = sb.tile([P, Q, PACK], BF16, name="q_bf", align_bytes=64)
+        g_bf = sb.tile([P, Q, PACK], BF16, name="g_bf", align_bytes=64)
+        q_words = sb.tile([P, Q], U32, name="q_words", align_bytes=64)
+        g_words = sb.tile([P, Q], U32, name="g_words", align_bytes=64)
+        q_scales = sb.tile([P, Q], U8, name="q_scales", align_bytes=64)
+        g_scales = sb.tile([P, Q], U8, name="g_scales", align_bytes=64)
+        nc.scalar.copy(q_bf[:], q_raw[:].rearrange("p j q -> p q j"))
         half4 = sb.tile([P, HALVES], F32, name="half4")
-        nc.gpsimd.tensor_scalar(half4[:], half_sb[:], 4.0, 0.0, ALU.mult, ALU.add)
+        columns_ps = ps.tile([P, P], F32, name="columns_ps", tag="bank_a")
+        nc.tensor.transpose(columns_ps[:], rows[:], ident[:])
+        nc.scalar.copy(columns[:], columns_ps[:, 0:2 * HALVES])
+        nc.scalar.activation(half4[:], columns_ps[:, HALVES:2 * HALVES], ACT.Copy, scale=4.0)
 
         va = [sb.tile([P, SLOTS], F32, name="va%d" % j) for j in range(PACK)]
         diff = [sb.tile([P, SLOTS], F32, name="diff%d" % j) for j in range(PACK)]
@@ -109,16 +116,17 @@ def tile_attend_bnovelty_pl_kernel(tc, query, keys_words, keys_scales, bias, hal
         base = sb.tile([P, HALVES], F32, name="base")
         for j in range(PACK):
             nc.vector.tensor_copy(va[j][:], vals_sb[j][:].indirect(list1[:]))
+            if j == 1:
+                nc.vector.quantize_mx(out=q_words[:].bitcast(FP8X4), scales=q_scales[:],
+                                      in_=q_bf[:].rearrange("p q j -> p (q j)"))
             if j == 2:
                 nc.vector.tensor_copy(ksg[:], ks[:].indirect(list1[:]))
             if j == 3:
                 nc.vector.tensor_copy(psg[:], pvs[:].indirect(list1[:]))
+                nc.scalar.copy(g_bf[:], g_raw[:].rearrange("p j q -> p q j"))
             nc.vector.tensor_tensor(diff[j][:], sval_sb[j][:].indirect(list2[:]), va[j][:], ALU.subtract)
             for h in range(HALVES):
                 nc.tensor.transpose(diff_t[h][:, j, :], diff[j][:, h * P:(h + 1) * P], ident[:])
-            if j == 0:
-                nc.vector.quantize_mx(out=qg_words[:].bitcast(FP8X4), scales=qg_scales[:],
-                                      in_=qg[:].rearrange("p a q j -> p (a q j)"))
             if j == 2:
                 for h in range(HALVES):
                     nc.scalar.activation(squares[:, 0:3 * P], diff_t[h][:, 0:3, :].rearrange("p j e -> p (j e)"),
@@ -126,6 +134,8 @@ def tile_attend_bnovelty_pl_kernel(tc, query, keys_words, keys_scales, bias, hal
                 for h in range(HALVES):
                     nc.scalar.activation(base[:, h:h + 1], early[:, h:h + 1], ACT.Identity,
                                          bias=half4[:, h:h + 1], scale=1.0 / 128.0)
+        nc.vector.quantize_mx(out=g_words[:].bitcast(FP8X4), scales=g_scales[:],
+                              in_=g_bf[:].rearrange("p q j -> p (q j)"))
         nc.vector.tensor_copy(kwg[:], kw[:].bitcast(U32).indirect(list1[:]))
 
         sumsq = sb.tile([P, HALVES], F32, name="sumsq")
@@ -136,11 +146,11 @@ def tile_attend_bnovelty_pl_kernel(tc, query, keys_words, keys_scales, bias, hal
             nc.scalar.activation(denom[:, h:h + 1], sumsq[:, h:h + 1], ACT.Square,
                                  bias=base[:, h:h + 1], scale=1.0 / 128.0)
 
-        score = ps.tile([P, HALVES, Q], F32, name="score")
+        score = ps.tile([P, HALVES, Q], F32, name="score", tag="bank_b")
         for h in range(HALVES):
             nc.tensor.matmul_mx(out=score[:, h, :], lhsT=kwg[:, h * P:(h + 1) * P].bitcast(FP8X4),
                                 lhsT_scale=ksg[:, h * P:(h + 1) * P],
-                                rhs=qg_words[:, 0:Q].bitcast(FP8X4), rhs_scale=qg_scales[:, 0:Q],
+                                rhs=q_words[:].bitcast(FP8X4), rhs_scale=q_scales[:],
                                 start=True, stop=True)
         gate = sb.tile([P, HALVES, Q], F32, name="gate")
         for h in range(HALVES):
@@ -149,7 +159,7 @@ def tile_attend_bnovelty_pl_kernel(tc, query, keys_words, keys_scales, bias, hal
         inv = sb.tile([P, HALVES], F32, name="inv")
         factor = sb.tile([P, HALVES], F32, name="factor")
         nc.vector.reciprocal(inv[:], denom[:])
-        nc.vector.tensor_tensor(factor[:], inv[:], half_sb[:], ALU.mult)
+        nc.vector.tensor_tensor(factor[:], inv[:], half_sb, ALU.mult)
 
         cols = SLOTS // 16 // HALVES
         dread = [ps.tile([P, Q], F32, name="dread%d" % h) for h in range(HALVES)]
@@ -158,18 +168,29 @@ def tile_attend_bnovelty_pl_kernel(tc, query, keys_words, keys_scales, bias, hal
                                   pw[:].bitcast(U32).indirect(list1[:, h * cols:(h + 1) * cols]))
             nc.tensor.matmul_mx(out=dread[h][:], lhsT=pwg[:, h * P:(h + 1) * P].bitcast(FP8X4),
                                 lhsT_scale=psg[:, h * P:(h + 1) * P],
-                                rhs=qg_words[:, Q:2 * Q].bitcast(FP8X4), rhs_scale=qg_scales[:, Q:2 * Q],
+                                rhs=g_words[:].bitcast(FP8X4), rhs_scale=g_scales[:],
                                 start=True, stop=True)
 
         terms = sb.tile([P, Q], F32, name="terms")
         coef = sb.tile([P, HALVES], F32, name="coef")
         coef_ps = [ps.tile([P, P], F32, name="coef_ps%d" % h) for h in range(HALVES)]
         coef_row = sb.tile([P, SLOTS], F32, name="coef_row")
+        grad_t = [sb.tile([P, PACK - 1, P], F32, name="grad_t%d" % h) for h in range(HALVES)]
+        grad1_ps = ps.tile([P, SLOTS], F32, name="grad1_ps", tag="bank_a")
+        grad23_ps = ps.tile([P, 2, SLOTS], F32, name="grad23_ps", tag="bank_b")
+        grad1 = sb.tile([P, SLOTS], F32, name="grad1")
+        grad23 = sb.tile([P, 2, SLOTS], F32, name="grad23")
         for h in range(HALVES):
             nc.vector.scalar_tensor_tensor(terms[:], dread[h][:], factor[:, h:h + 1], gate[:, h, :],
                                            ALU.mult, ALU.mult, accum_out=coef[:, h:h + 1])
             nc.tensor.transpose(coef_ps[h][:], coef[:, h:h + 1].to_broadcast([P, P]), ident[:])
             nc.scalar.copy(coef_row[:, h * P:(h + 1) * P], coef_ps[h][:])
+            nc.scalar.activation(grad_t[h][:], diff_t[h][:, 1:PACK, :], ACT.Copy, scale=coef[:, h:h + 1])
+            nc.tensor.transpose(grad1_ps[:, h * P:(h + 1) * P], grad_t[h][:, 0, :], ident[:])
+            for j in range(2):
+                nc.tensor.transpose(grad23_ps[:, j, h * P:(h + 1) * P], grad_t[h][:, 1 + j, :], ident[:])
+        nc.scalar.copy(grad1[:], grad1_ps[:])
+        nc.scalar.copy(grad23[:], grad23_ps[:])
 
         yq = [sb.tile([P, c1 - c0, PACK], BF16, name="yq%d" % c0, align_bytes=64) for c0, c1 in CHUNKS]
         words = [sb.tile([P, c1 - c0], U32, name="words%d" % c0, align_bytes=64) for c0, c1 in CHUNKS]
@@ -177,19 +198,19 @@ def tile_attend_bnovelty_pl_kernel(tc, query, keys_words, keys_scales, bias, hal
         out_planes = planes(out_0)
         out_bytes = out_1[0].rearrange("p n t -> p (n t)")
 
+        for h in range(HALVES):
+            nc.vector.tensor_tensor(gf[0][:].indirect(list2[:, h * cols:(h + 1) * cols]),
+                                    diff[0][:, h * P:(h + 1) * P], coef_row[:, h * P:(h + 1) * P], ALU.mult)
+        nc.vector.tensor_copy(gf[1][:].indirect(list2[:]), grad1[:])
         for j in range(2):
-            if j == 0:
-                for h in range(HALVES):
-                    nc.vector.tensor_tensor(gf[j][:].indirect(list2[:, h * cols:(h + 1) * cols]),
-                                            diff[j][:, h * P:(h + 1) * P], coef_row[:, h * P:(h + 1) * P], ALU.mult)
-            else:
-                nc.vector.tensor_tensor(gf[j][:].indirect(list2[:]), diff[j][:], coef_row[:], ALU.mult)
-            nc.vector.tensor_tensor(y[0][:, j, :], y[0][:, j, :], gf[j][:], ALU.add)
-            nc.sync.dma_start(out_planes[:, j, :], y[0][:, j, :])
+            nc.vector.tensor_copy(gf[2 + j][:].indirect(list2[:]), grad23[:, j, :])
+        nc.gpsimd.tensor_tensor(y[0][:, 0, :], y[0][:, 0, :], gf[0][:], ALU.add)
+        nc.sync.dma_start(out_planes[:, 0, :], y[0][:, 0, :])
         for n, (c0, c1) in enumerate(CHUNKS):
+            nc.gpsimd.tensor_tensor(y[0][:, 1, c0:c1], y[0][:, 1, c0:c1], gf[1][:, c0:c1], ALU.add)
             nc.scalar.copy(yq[n][:, :, 0:2], y[0][:, :, c0:c1].rearrange("p j t -> p t j"))
-        for j in range(2, 4):
-            nc.vector.tensor_tensor(gf[j][:].indirect(list2[:]), diff[j][:], coef_row[:], ALU.mult)
+            if n % 2 == 1:
+                nc.sync.dma_start(out_planes[:, 1, c1 - 512:c1], y[0][:, 1, c1 - 512:c1])
 
         def quantise(n):
             c0, c1 = CHUNKS[n]
@@ -197,14 +218,18 @@ def tile_attend_bnovelty_pl_kernel(tc, query, keys_words, keys_scales, bias, hal
                                   in_=yq[n][:].rearrange("p t j -> p (t j)"))
             nc.sync.dma_start(out_bytes[:, PACK * c0:PACK * c1].bitcast(I32), words[n][:].bitcast(I32))
 
+        nc.vector.tensor_tensor(y[1][:, 0, :], y[1][:, 0, :], gf[2][:], ALU.add)
+        nc.sync.dma_start(out_planes[:, 2, :], y[1][:, 0, :])
         for n, (c0, c1) in enumerate(CHUNKS):
-            for j in range(2):
-                nc.vector.tensor_tensor(y[1][:, j, c0:c1], y[1][:, j, c0:c1], gf[2 + j][:, c0:c1], ALU.add)
-            nc.scalar.copy(yq[n][:, :, 2:4], y[1][:, :, c0:c1].rearrange("p j t -> p t j"))
-            nc.sync.dma_start(out_planes[:, 2:4, c0:c1], y[1][:, :, c0:c1])
-            if n > 0:
-                quantise(n - 1)
-        quantise(len(CHUNKS) - 1)
+            nc.vector.tensor_tensor(y[1][:, 1, c0:c1], y[1][:, 1, c0:c1], gf[3][:, c0:c1], ALU.add)
+            if n < 3:
+                nc.scalar.copy(yq[n][:, :, 2:4], y[1][:, :, c0:c1].rearrange("p j t -> p t j"))
+            if n % 2 == 1:
+                nc.sync.dma_start(out_planes[:, 3, c1 - 512:c1], y[1][:, 1, c1 - 512:c1])
+        quantise(0)
+        nc.vector.tensor_copy(yq[3][:, :, 2:4], y[1][:, :, 768:1024].rearrange("p j t -> p t j"))
+        for n in (1, 3, 2):
+            quantise(n)
         for quad in range(4):
             queue = nc.sync if quad % 2 == 0 else nc.scalar
             queue.dma_start(out_2[0, 4 * quad:4 * quad + 4, :].bitcast(I32),

@@ -54,38 +54,41 @@ def tile_attend_bnovelty_pl_kernel(tc, query, keys_words, keys_scales, bias, hal
         warm_in = sb.tile([P, 1], F32, name="warm_in")
         warm_out = sb.tile([P, 1], F32, name="warm_out")
 
+        nc.gpsimd.memset(rows[:], 0.0)
         nc.gpsimd.memset(ks[:].bitcast(I32), 0)
         nc.gpsimd.memset(pvs[:].bitcast(I32), 0)
         nc.gpsimd.memset(warm_in[:], 0.0)
-        nc.gpsimd.memset(rows[:], 0.0)
         nc.scalar.activation(warm_out[:], warm_in[:], ACT.Sigmoid)
         make_identity(nc, ident[:])
         for j in range(PACK):
             engine = nc.vector if j < 2 else nc.gpsimd
             engine.memset(gf[j][:], 0.0)
 
-        def load_scale_rows(tile, src, quad):
-            nc.sync.dma_start(tile[32 * quad:32 * quad + 4, :].bitcast(I32),
-                              src[0, 4 * quad:4 * quad + 4, :].bitcast(I32))
+        def load_scale_rows(tile, src, r):
+            nc.sync.dma_start(tile[r:P:32, :].bitcast(I32), src[0, r:16:4, :].bitcast(I32))
 
         nc.sync.dma_start(vals_sb[0][:], planes(vals)[:, 0, :])
         nc.sync.dma_start(list1[:], offs)
+        nc.sync.dma_start(sval_sb[0][:], planes(sval)[:, 0, :])
         nc.sync.dma_start(list2[:], offs2)
-        big = [(sval_sb[0], planes(sval)[:, 0, :])]
-        for j in range(1, PACK):
-            big = big + [(vals_sb[j], planes(vals)[:, j, :]), (sval_sb[j], planes(sval)[:, j, :])]
-        small = [(ks, keys_scales, quad) for quad in range(4)] + [(pvs, pv_scales, quad) for quad in range(4)]
-        for n, (tile, src) in enumerate(big):
-            nc.sync.dma_start(tile[:], src)
-            if n < 4:
-                load_scale_rows(*small[2 * n])
-                load_scale_rows(*small[2 * n + 1])
-            if n == 0:
-                nc.sync.dma_start(q_raw[:], planes(query))
-            if n == 4:
-                nc.sync.dma_start(rows[0:HALVES, :], bias.rearrange("(h p) o -> h (p o)", p=P))
-                nc.sync.dma_start(rows[HALVES:2 * HALVES, :], half.rearrange("(h p) o -> h (p o)", p=P))
+        nc.sync.dma_start(vals_sb[1][:], planes(vals)[:, 1, :])
+        nc.sync.dma_start(rows[HALVES:2 * HALVES, :], half.rearrange("(h p) o -> h (p o)", p=P))
+        nc.sync.dma_start(q_raw[:], planes(query))
+        nc.sync.dma_start(rows[0:HALVES, :], bias.rearrange("(h p) o -> h (p o)", p=P))
+        nc.sync.dma_start(sval_sb[1][:], planes(sval)[:, 1, :])
+        load_scale_rows(ks, keys_scales, 0)
+        nc.sync.dma_start(vals_sb[2][:], planes(vals)[:, 2, :])
+        load_scale_rows(ks, keys_scales, 1)
+        nc.sync.dma_start(sval_sb[2][:], planes(sval)[:, 2, :])
+        load_scale_rows(ks, keys_scales, 2)
+        load_scale_rows(ks, keys_scales, 3)
+        nc.sync.dma_start(vals_sb[3][:], planes(vals)[:, 3, :])
+        load_scale_rows(pvs, pv_scales, 0)
+        nc.sync.dma_start(sval_sb[3][:], planes(sval)[:, 3, :])
+        load_scale_rows(pvs, pv_scales, 1)
         nc.sync.dma_start(g_raw[:], planes(gout))
+        load_scale_rows(pvs, pv_scales, 2)
+        load_scale_rows(pvs, pv_scales, 3)
         nc.sync.dma_start(kw[:], keys_words[0].rearrange("p n t -> p (n t)").bitcast(I32))
         nc.sync.dma_start(pw[:], pv_words[0].rearrange("p n t -> p (n t)").bitcast(I32))
         for j in range(PACK):
@@ -104,25 +107,23 @@ def tile_attend_bnovelty_pl_kernel(tc, query, keys_words, keys_scales, bias, hal
         nc.scalar.copy(columns[:], columns_ps[:, 0:2 * HALVES])
         nc.scalar.activation(half4[:], columns_ps[:, HALVES:2 * HALVES], ACT.Copy, scale=4.0)
 
-        va = [sb.tile([P, SLOTS], F32, name="va%d" % j) for j in range(PACK)]
+        va = [sb.tile([P, SLOTS], F32, name="va%d" % j, align_bytes=64) for j in range(PACK)]
         diff = [sb.tile([P, SLOTS], F32, name="diff%d" % j) for j in range(PACK)]
         diff_t = [ps.tile([P, PACK, P], F32, name="diff_t%d" % h) for h in range(HALVES)]
-        ksg = sb.tile([P, SLOTS], U8, name="ksg", align_bytes=64)
-        psg = sb.tile([P, SLOTS], U8, name="psg", align_bytes=64)
         kwg = sb.tile([P, SLOTS], U32, name="kwg", align_bytes=64)
         pwg = sb.tile([P, SLOTS], U32, name="pwg", align_bytes=64)
         squares = sb.tile([P, 3 * P], F32, name="squares")
         early = sb.tile([P, HALVES], F32, name="early")
         base = sb.tile([P, HALVES], F32, name="base")
         for j in range(PACK):
+            if j == 3:
+                ksg = sb.tile([P, SLOTS], U8, name="ksg", tag="va2", align_bytes=64)
+                nc.vector.tensor_copy(ksg[:], ks[:].indirect(list1[:]))
             nc.vector.tensor_copy(va[j][:], vals_sb[j][:].indirect(list1[:]))
             if j == 1:
                 nc.vector.quantize_mx(out=q_words[:].bitcast(FP8X4), scales=q_scales[:],
                                       in_=q_bf[:].rearrange("p q j -> p (q j)"))
-            if j == 2:
-                nc.vector.tensor_copy(ksg[:], ks[:].indirect(list1[:]))
             if j == 3:
-                nc.vector.tensor_copy(psg[:], pvs[:].indirect(list1[:]))
                 nc.scalar.copy(g_bf[:], g_raw[:].rearrange("p j q -> p q j"))
             nc.vector.tensor_tensor(diff[j][:], sval_sb[j][:].indirect(list2[:]), va[j][:], ALU.subtract)
             for h in range(HALVES):
@@ -134,14 +135,17 @@ def tile_attend_bnovelty_pl_kernel(tc, query, keys_words, keys_scales, bias, hal
                 for h in range(HALVES):
                     nc.scalar.activation(base[:, h:h + 1], early[:, h:h + 1], ACT.Identity,
                                          bias=half4[:, h:h + 1], scale=1.0 / 128.0)
+        psg = sb.tile([P, SLOTS], U8, name="psg", tag="va3", align_bytes=64)
+        nc.vector.tensor_copy(psg[:], pvs[:].indirect(list1[:]))
         nc.vector.quantize_mx(out=g_words[:].bitcast(FP8X4), scales=g_scales[:],
                               in_=g_bf[:].rearrange("p q j -> p (q j)"))
         nc.vector.tensor_copy(kwg[:], kw[:].bitcast(U32).indirect(list1[:]))
 
         sumsq = sb.tile([P, HALVES], F32, name="sumsq")
         denom = sb.tile([P, HALVES], F32, name="denom")
+        late_squares = sb.tile([P, P], F32, name="late_squares", tag="g_raw")
         for h in range(HALVES):
-            nc.scalar.activation(squares[:, 0:P], diff_t[h][:, 3, :], ACT.Square, accum_out=sumsq[:, h:h + 1])
+            nc.scalar.activation(late_squares[:], diff_t[h][:, 3, :], ACT.Square, accum_out=sumsq[:, h:h + 1])
         for h in range(HALVES):
             nc.scalar.activation(denom[:, h:h + 1], sumsq[:, h:h + 1], ACT.Square,
                                  bias=base[:, h:h + 1], scale=1.0 / 128.0)
@@ -156,7 +160,7 @@ def tile_attend_bnovelty_pl_kernel(tc, query, keys_words, keys_scales, bias, hal
         for h in range(HALVES):
             nc.scalar.activation(gate[:, h, :], score[:, h, :], ACT.Sigmoid, bias=bias_sb[:, h:h + 1])
 
-        inv = sb.tile([P, HALVES], F32, name="inv")
+        inv = sb.tile([P, HALVES], F32, name="inv", tag="kw")
         factor = sb.tile([P, HALVES], F32, name="factor")
         nc.vector.reciprocal(inv[:], denom[:])
         nc.vector.tensor_tensor(factor[:], inv[:], half_sb, ALU.mult)
@@ -175,62 +179,73 @@ def tile_attend_bnovelty_pl_kernel(tc, query, keys_words, keys_scales, bias, hal
         coef = sb.tile([P, HALVES], F32, name="coef")
         coef_ps = [ps.tile([P, P], F32, name="coef_ps%d" % h) for h in range(HALVES)]
         coef_row = sb.tile([P, SLOTS], F32, name="coef_row")
-        grad_t = [sb.tile([P, PACK - 1, P], F32, name="grad_t%d" % h) for h in range(HALVES)]
-        grad1_ps = ps.tile([P, SLOTS], F32, name="grad1_ps", tag="bank_a")
-        grad23_ps = ps.tile([P, 2, SLOTS], F32, name="grad23_ps", tag="bank_b")
-        grad1 = sb.tile([P, SLOTS], F32, name="grad1")
-        grad23 = sb.tile([P, 2, SLOTS], F32, name="grad23")
         for h in range(HALVES):
             nc.vector.scalar_tensor_tensor(terms[:], dread[h][:], factor[:, h:h + 1], gate[:, h, :],
                                            ALU.mult, ALU.mult, accum_out=coef[:, h:h + 1])
             nc.tensor.transpose(coef_ps[h][:], coef[:, h:h + 1].to_broadcast([P, P]), ident[:])
             nc.scalar.copy(coef_row[:, h * P:(h + 1) * P], coef_ps[h][:])
-            nc.scalar.activation(grad_t[h][:], diff_t[h][:, 1:PACK, :], ACT.Copy, scale=coef[:, h:h + 1])
-            nc.tensor.transpose(grad1_ps[:, h * P:(h + 1) * P], grad_t[h][:, 0, :], ident[:])
-            for j in range(2):
-                nc.tensor.transpose(grad23_ps[:, j, h * P:(h + 1) * P], grad_t[h][:, 1 + j, :], ident[:])
-        nc.scalar.copy(grad1[:], grad1_ps[:])
-        nc.scalar.copy(grad23[:], grad23_ps[:])
 
         yq = [sb.tile([P, c1 - c0, PACK], BF16, name="yq%d" % c0, align_bytes=64) for c0, c1 in CHUNKS]
-        words = [sb.tile([P, c1 - c0], U32, name="words%d" % c0, align_bytes=64) for c0, c1 in CHUNKS]
+        words = sb.tile([P, T], U32, name="words", align_bytes=64)
         scales = sb.tile([P, T], U8, name="scales", align_bytes=64)
         out_planes = planes(out_0)
         out_bytes = out_1[0].rearrange("p n t -> p (n t)")
 
-        for h in range(HALVES):
-            nc.vector.tensor_tensor(gf[0][:].indirect(list2[:, h * cols:(h + 1) * cols]),
-                                    diff[0][:, h * P:(h + 1) * P], coef_row[:, h * P:(h + 1) * P], ALU.mult)
-        nc.vector.tensor_copy(gf[1][:].indirect(list2[:]), grad1[:])
-        for j in range(2):
-            nc.vector.tensor_copy(gf[2 + j][:].indirect(list2[:]), grad23[:, j, :])
-        nc.gpsimd.tensor_tensor(y[0][:, 0, :], y[0][:, 0, :], gf[0][:], ALU.add)
-        nc.sync.dma_start(out_planes[:, 0, :], y[0][:, 0, :])
-        for n, (c0, c1) in enumerate(CHUNKS):
-            nc.gpsimd.tensor_tensor(y[0][:, 1, c0:c1], y[0][:, 1, c0:c1], gf[1][:, c0:c1], ALU.add)
-            nc.scalar.copy(yq[n][:, :, 0:2], y[0][:, :, c0:c1].rearrange("p j t -> p t j"))
-            if n % 2 == 1:
-                nc.sync.dma_start(out_planes[:, 1, c1 - 512:c1], y[0][:, 1, c1 - 512:c1])
+        def scatter(j, h0, h1):
+            nc.vector.tensor_tensor(gf[j][:].indirect(list2[:, h0 * cols:h1 * cols]),
+                                    diff[j][:, h0 * P:h1 * P], coef_row[:, h0 * P:h1 * P], ALU.mult)
+
+        def add(j, c0, c1):
+            part = y[j // 2][:, j % 2, c0:c1]
+            nc.vector.tensor_tensor(part, part, gf[j][:, c0:c1], ALU.add)
+
+        def store(j, c0, c1):
+            nc.sync.dma_start(out_planes[:, j, c0:c1], y[j // 2][:, j % 2, c0:c1])
+
+        def cast(copy, pair, n):
+            c0, c1 = CHUNKS[n]
+            copy(yq[n][:, :, 2 * pair:2 * pair + 2], y[pair][:, :, c0:c1].rearrange("p j t -> p t j"))
 
         def quantise(n):
             c0, c1 = CHUNKS[n]
-            nc.vector.quantize_mx(out=words[n][:].bitcast(FP8X4), scales=scales[:, c0:c1],
+            nc.vector.quantize_mx(out=words[:, c0:c1].bitcast(FP8X4), scales=scales[:, c0:c1],
                                   in_=yq[n][:].rearrange("p t j -> p (t j)"))
-            nc.sync.dma_start(out_bytes[:, PACK * c0:PACK * c1].bitcast(I32), words[n][:].bitcast(I32))
 
-        nc.vector.tensor_tensor(y[1][:, 0, :], y[1][:, 0, :], gf[2][:], ALU.add)
-        nc.sync.dma_start(out_planes[:, 2, :], y[1][:, 0, :])
-        for n, (c0, c1) in enumerate(CHUNKS):
-            nc.vector.tensor_tensor(y[1][:, 1, c0:c1], y[1][:, 1, c0:c1], gf[3][:, c0:c1], ALU.add)
-            if n < 3:
-                nc.scalar.copy(yq[n][:, :, 2:4], y[1][:, :, c0:c1].rearrange("p j t -> p t j"))
-            if n % 2 == 1:
-                nc.sync.dma_start(out_planes[:, 3, c1 - 512:c1], y[1][:, 1, c1 - 512:c1])
+        def store_words(c0, c1):
+            nc.sync.dma_start(out_bytes[:, PACK * c0:PACK * c1].bitcast(I32), words[:, c0:c1].bitcast(I32))
+
+        scatter(0, 0, 1)
+        scatter(0, 1, 2)
+        scatter(1, 0, 2)
+        for j in range(2):
+            add(j, 0, T)
+            store(j, 0, T)
+        for n in range(len(CHUNKS)):
+            cast(nc.scalar.copy, 0, n)
+        scatter(2, 0, 2)
+        scatter(3, 0, 1)
+        add(2, 0, 512)
+        store(2, 0, 512)
+        scatter(3, 1, 2)
+        add(2, 512, 768)
+        for n in range(2):
+            add(3, *CHUNKS[n])
+            cast(nc.scalar.copy, 1, n)
+        store(3, 0, 512)
+        add(2, 768, T)
+        store(2, 512, T)
+        add(3, *CHUNKS[2])
+        cast(nc.scalar.copy, 1, 2)
+        add(3, *CHUNKS[3])
+        store(3, 512, T)
         quantise(0)
-        nc.vector.tensor_copy(yq[3][:, :, 2:4], y[1][:, :, 768:1024].rearrange("p j t -> p t j"))
-        for n in (1, 3, 2):
-            quantise(n)
-        for quad in range(4):
-            queue = nc.sync if quad % 2 == 0 else nc.scalar
-            queue.dma_start(out_2[0, 4 * quad:4 * quad + 4, :].bitcast(I32),
-                            scales[32 * quad:32 * quad + 4, :].bitcast(I32))
+        cast(nc.vector.tensor_copy, 1, 3)
+        quantise(1)
+        store_words(0, 512)
+        quantise(3)
+        store_words(768, T)
+        quantise(2)
+        store_words(512, 768)
+        for r in range(4):
+            queue = nc.sync if r % 2 == 0 else nc.scalar
+            queue.dma_start(out_2[0, r:16:4, :].bitcast(I32), scales[r:P:32, :].bitcast(I32))

from contextlib import ExitStack

import concourse.mybir as mybir
from concourse.masks import make_identity

F32 = mybir.dt.float32
BF16 = mybir.dt.bfloat16
I32 = mybir.dt.int32
U32 = mybir.dt.uint32
U16 = mybir.dt.uint16
U8 = mybir.dt.uint8
FP8X4 = mybir.dt.float8_e4m3fn_x4
ALU = mybir.AluOpType
ACT = mybir.ActivationFunctionType

P = 128
PACK = 4
T = 1024
SLOTS = 256
Q = 128
HALVES = SLOTS // P
CHUNKS = [(0, 256), (256, 512), (512, 768), (768, 1024)]

FLOPS = 2 * 2 * 512 * SLOTS * Q


def tile_attend_bnovelty_pl_kernel(tc, query, keys_words, keys_scales, bias, half, vals, sval, gout,
                                    pv_words, pv_scales, old, offs, offs2, out_0, out_1, out_2):
    nc = tc.nc
    with ExitStack() as ctx:
        sb = ctx.enter_context(tc.tile_pool(name="sb", bufs=1))
        ps = ctx.enter_context(tc.psum_pool(name="ps", bufs=1))

        def planes(x):
            return x.rearrange("(p j) t -> p j t", j=PACK)

        list1 = sb.tile([P, SLOTS // 16], U16, name="list1")
        list2 = sb.tile([P, SLOTS // 16], U16, name="list2")
        vals_sb = [sb.tile([P, T], F32, name="vals%d" % j) for j in range(PACK)]
        sval_sb = [sb.tile([P, T], F32, name="sval%d" % j) for j in range(PACK)]
        gf = [sb.tile([P, T], F32, name="gf%d" % j) for j in range(PACK)]
        y = [sb.tile([P, 2, T], F32, name="y%d" % u) for u in range(2)]
        q_raw = sb.tile([P, PACK, Q], F32, name="q_raw")
        g_raw = sb.tile([P, PACK, Q], F32, name="g_raw")
        rows = sb.tile([P, P], F32, name="rows")
        columns = sb.tile([P, 2 * HALVES], F32, name="columns")
        bias_sb = columns[:, 0:HALVES]
        half_sb = columns[:, HALVES:2 * HALVES]
        kw = sb.tile([P, T], I32, name="kw")
        pw = sb.tile([P, T], I32, name="pw")
        ks = sb.tile([P, T], U8, name="ks")
        pvs = sb.tile([P, T], U8, name="pvs")
        ident = sb.tile([P, P], F32, name="ident")
        warm_in = sb.tile([P, 1], F32, name="warm_in")
        warm_out = sb.tile([P, 1], F32, name="warm_out")

        nc.gpsimd.memset(rows[:], 0.0)
        nc.gpsimd.memset(ks[:].bitcast(I32), 0)
        nc.gpsimd.memset(pvs[:].bitcast(I32), 0)
        nc.gpsimd.memset(warm_in[:], 0.0)
        nc.scalar.activation(warm_out[:], warm_in[:], ACT.Sigmoid)
        make_identity(nc, ident[:])
        for j in range(PACK):
            engine = nc.vector if j < 2 else nc.gpsimd
            engine.memset(gf[j][:], 0.0)

        def load_scale_rows(tile, src, r):
            nc.sync.dma_start(tile[r:P:32, :].bitcast(I32), src[0, r:16:4, :].bitcast(I32))

        nc.sync.dma_start(vals_sb[0][:], planes(vals)[:, 0, :])
        nc.sync.dma_start(list1[:], offs)
        nc.sync.dma_start(sval_sb[0][:], planes(sval)[:, 0, :])
        nc.sync.dma_start(list2[:], offs2)
        nc.sync.dma_start(vals_sb[1][:], planes(vals)[:, 1, :])
        nc.sync.dma_start(rows[HALVES:2 * HALVES, :], half.rearrange("(h p) o -> h (p o)", p=P))
        nc.sync.dma_start(q_raw[:], planes(query))
        nc.sync.dma_start(rows[0:HALVES, :], bias.rearrange("(h p) o -> h (p o)", p=P))
        nc.sync.dma_start(sval_sb[1][:], planes(sval)[:, 1, :])
        load_scale_rows(ks, keys_scales, 0)
        nc.sync.dma_start(vals_sb[2][:], planes(vals)[:, 2, :])
        load_scale_rows(ks, keys_scales, 1)
        nc.sync.dma_start(sval_sb[2][:], planes(sval)[:, 2, :])
        load_scale_rows(ks, keys_scales, 2)
        load_scale_rows(ks, keys_scales, 3)
        nc.sync.dma_start(vals_sb[3][:], planes(vals)[:, 3, :])
        load_scale_rows(pvs, pv_scales, 0)
        nc.sync.dma_start(sval_sb[3][:], planes(sval)[:, 3, :])
        load_scale_rows(pvs, pv_scales, 1)
        nc.sync.dma_start(g_raw[:], planes(gout))
        load_scale_rows(pvs, pv_scales, 2)
        load_scale_rows(pvs, pv_scales, 3)
        nc.sync.dma_start(kw[:], keys_words[0].rearrange("p n t -> p (n t)").bitcast(I32))
        nc.sync.dma_start(pw[:], pv_words[0].rearrange("p n t -> p (n t)").bitcast(I32))
        for j in range(PACK):
            nc.sync.dma_start(y[j // 2][:, j % 2, :], planes(old)[:, j, :])

        q_bf = sb.tile([P, Q, PACK], BF16, name="q_bf", align_bytes=64)
        g_bf = sb.tile([P, Q, PACK], BF16, name="g_bf", align_bytes=64)
        q_words = sb.tile([P, Q], U32, name="q_words", align_bytes=64)
        g_words = sb.tile([P, Q], U32, name="g_words", align_bytes=64)
        q_scales = sb.tile([P, Q], U8, name="q_scales", align_bytes=64)
        g_scales = sb.tile([P, Q], U8, name="g_scales", align_bytes=64)
        nc.scalar.copy(q_bf[:], q_raw[:].rearrange("p j q -> p q j"))
        half4 = sb.tile([P, HALVES], F32, name="half4")
        columns_ps = ps.tile([P, P], F32, name="columns_ps", tag="bank_a")
        nc.tensor.transpose(columns_ps[:], rows[:], ident[:])
        nc.scalar.copy(columns[:], columns_ps[:, 0:2 * HALVES])
        nc.scalar.activation(half4[:], columns_ps[:, HALVES:2 * HALVES], ACT.Copy, scale=4.0)

        va = [sb.tile([P, SLOTS], F32, name="va%d" % j, align_bytes=64) for j in range(PACK)]
        diff = [sb.tile([P, SLOTS], F32, name="diff%d" % j) for j in range(PACK)]
        diff_t = [ps.tile([P, PACK, P], F32, name="diff_t%d" % h) for h in range(HALVES)]
        kwg = sb.tile([P, SLOTS], U32, name="kwg", align_bytes=64)
        pwg = sb.tile([P, SLOTS], U32, name="pwg", align_bytes=64)
        squares = sb.tile([P, 3 * P], F32, name="squares")
        early = sb.tile([P, HALVES], F32, name="early")
        base = sb.tile([P, HALVES], F32, name="base")
        for j in range(PACK):
            if j == 3:
                ksg = sb.tile([P, SLOTS], U8, name="ksg", tag="va2", align_bytes=64)
                nc.vector.tensor_copy(ksg[:], ks[:].indirect(list1[:]))
            nc.vector.tensor_copy(va[j][:], vals_sb[j][:].indirect(list1[:]))
            if j == 1:
                nc.vector.quantize_mx(out=q_words[:].bitcast(FP8X4), scales=q_scales[:],
                                      in_=q_bf[:].rearrange("p q j -> p (q j)"))
            if j == 3:
                nc.scalar.copy(g_bf[:], g_raw[:].rearrange("p j q -> p q j"))
            nc.vector.tensor_tensor(diff[j][:], sval_sb[j][:].indirect(list2[:]), va[j][:], ALU.subtract)
            for h in range(HALVES):
                nc.tensor.transpose(diff_t[h][:, j, :], diff[j][:, h * P:(h + 1) * P], ident[:])
            if j == 2:
                for h in range(HALVES):
                    nc.scalar.activation(squares[:, 0:3 * P], diff_t[h][:, 0:3, :].rearrange("p j e -> p (j e)"),
                                         ACT.Square, accum_out=early[:, h:h + 1])
                for h in range(HALVES):
                    nc.scalar.activation(base[:, h:h + 1], early[:, h:h + 1], ACT.Identity,
                                         bias=half4[:, h:h + 1], scale=1.0 / 128.0)
        psg = sb.tile([P, SLOTS], U8, name="psg", tag="va3", align_bytes=64)
        nc.vector.tensor_copy(psg[:], pvs[:].indirect(list1[:]))
        nc.vector.quantize_mx(out=g_words[:].bitcast(FP8X4), scales=g_scales[:],
                              in_=g_bf[:].rearrange("p q j -> p (q j)"))
        nc.vector.tensor_copy(kwg[:], kw[:].bitcast(U32).indirect(list1[:]))

        sumsq = sb.tile([P, HALVES], F32, name="sumsq")
        denom = sb.tile([P, HALVES], F32, name="denom")
        late_squares = sb.tile([P, P], F32, name="late_squares", tag="g_raw")
        for h in range(HALVES):
            nc.scalar.activation(late_squares[:], diff_t[h][:, 3, :], ACT.Square, accum_out=sumsq[:, h:h + 1])
        for h in range(HALVES):
            nc.scalar.activation(denom[:, h:h + 1], sumsq[:, h:h + 1], ACT.Square,
                                 bias=base[:, h:h + 1], scale=1.0 / 128.0)

        score = ps.tile([P, HALVES, Q], F32, name="score", tag="bank_b")
        for h in range(HALVES):
            nc.tensor.matmul_mx(out=score[:, h, :], lhsT=kwg[:, h * P:(h + 1) * P].bitcast(FP8X4),
                                lhsT_scale=ksg[:, h * P:(h + 1) * P],
                                rhs=q_words[:].bitcast(FP8X4), rhs_scale=q_scales[:],
                                start=True, stop=True)
        gate = sb.tile([P, HALVES, Q], F32, name="gate")
        for h in range(HALVES):
            nc.scalar.activation(gate[:, h, :], score[:, h, :], ACT.Sigmoid, bias=bias_sb[:, h:h + 1])

        inv = sb.tile([P, HALVES], F32, name="inv", tag="kw")
        factor = sb.tile([P, HALVES], F32, name="factor")
        nc.vector.reciprocal(inv[:], denom[:])
        nc.vector.tensor_tensor(factor[:], inv[:], half_sb, ALU.mult)

        cols = SLOTS // 16 // HALVES
        dread = [ps.tile([P, Q], F32, name="dread%d" % h) for h in range(HALVES)]
        for h in range(HALVES):
            nc.vector.tensor_copy(pwg[:, h * P:(h + 1) * P],
                                  pw[:].bitcast(U32).indirect(list1[:, h * cols:(h + 1) * cols]))
            nc.tensor.matmul_mx(out=dread[h][:], lhsT=pwg[:, h * P:(h + 1) * P].bitcast(FP8X4),
                                lhsT_scale=psg[:, h * P:(h + 1) * P],
                                rhs=g_words[:].bitcast(FP8X4), rhs_scale=g_scales[:],
                                start=True, stop=True)

        terms = sb.tile([P, Q], F32, name="terms")
        coef = sb.tile([P, HALVES], F32, name="coef")
        coef_ps = [ps.tile([P, P], F32, name="coef_ps%d" % h) for h in range(HALVES)]
        coef_row = sb.tile([P, SLOTS], F32, name="coef_row")
        for h in range(HALVES):
            nc.vector.scalar_tensor_tensor(terms[:], dread[h][:], factor[:, h:h + 1], gate[:, h, :],
                                           ALU.mult, ALU.mult, accum_out=coef[:, h:h + 1])
            nc.tensor.transpose(coef_ps[h][:], coef[:, h:h + 1].to_broadcast([P, P]), ident[:])
            nc.scalar.copy(coef_row[:, h * P:(h + 1) * P], coef_ps[h][:])

        yq = [sb.tile([P, c1 - c0, PACK], BF16, name="yq%d" % c0, align_bytes=64) for c0, c1 in CHUNKS]
        words = sb.tile([P, T], U32, name="words", align_bytes=64)
        scales = sb.tile([P, T], U8, name="scales", align_bytes=64)
        out_planes = planes(out_0)
        out_bytes = out_1[0].rearrange("p n t -> p (n t)")

        def scatter(j, h0, h1):
            nc.vector.tensor_tensor(gf[j][:].indirect(list2[:, h0 * cols:h1 * cols]),
                                    diff[j][:, h0 * P:h1 * P], coef_row[:, h0 * P:h1 * P], ALU.mult)

        def add(j, c0, c1):
            part = y[j // 2][:, j % 2, c0:c1]
            nc.vector.tensor_tensor(part, part, gf[j][:, c0:c1], ALU.add)

        def store(j, c0, c1):
            nc.sync.dma_start(out_planes[:, j, c0:c1], y[j // 2][:, j % 2, c0:c1])

        def cast(copy, pair, n):
            c0, c1 = CHUNKS[n]
            copy(yq[n][:, :, 2 * pair:2 * pair + 2], y[pair][:, :, c0:c1].rearrange("p j t -> p t j"))

        def quantise(n):
            c0, c1 = CHUNKS[n]
            nc.vector.quantize_mx(out=words[:, c0:c1].bitcast(FP8X4), scales=scales[:, c0:c1],
                                  in_=yq[n][:].rearrange("p t j -> p (t j)"))

        def store_words(c0, c1):
            nc.sync.dma_start(out_bytes[:, PACK * c0:PACK * c1].bitcast(I32), words[:, c0:c1].bitcast(I32))

        scatter(0, 0, 1)
        scatter(0, 1, 2)
        scatter(1, 0, 2)
        for j in range(2):
            add(j, 0, T)
            store(j, 0, T)
        for n in range(len(CHUNKS)):
            cast(nc.scalar.copy, 0, n)
        scatter(2, 0, 2)
        scatter(3, 0, 1)
        add(2, 0, 512)
        store(2, 0, 512)
        scatter(3, 1, 2)
        add(2, 512, 768)
        for n in range(2):
            add(3, *CHUNKS[n])
            cast(nc.scalar.copy, 1, n)
        store(3, 0, 512)
        add(2, 768, T)
        store(2, 512, T)
        add(3, *CHUNKS[2])
        cast(nc.scalar.copy, 1, 2)
        add(3, *CHUNKS[3])
        store(3, 512, T)
        quantise(0)
        cast(nc.vector.tensor_copy, 1, 3)
        quantise(1)
        store_words(0, 512)
        quantise(3)
        store_words(768, T)
        quantise(2)
        store_words(512, 768)
        for r in range(4):
            queue = nc.sync if r % 2 == 0 else nc.scalar
            queue.dma_start(out_2[0, r:16:4, :].bitcast(I32), scales[r:P:32, :].bitcast(I32))
